import numpy as np
import ml_dtypes


def mxq(x, axis, fmt="e4m3"):
    dtype, down = {"e4m3": (ml_dtypes.float8_e4m3fn, 7), "e5m2": (ml_dtypes.float8_e5m2, 14)}[fmt]
    v = np.moveaxis(np.asarray(x, np.float32).astype(ml_dtypes.bfloat16).astype(np.float64), axis, -1)
    blocks = v.reshape(v.shape[:-1] + (-1, 32))
    amax = np.abs(blocks).max(-1, keepdims=True)
    byte = np.maximum(np.where(amax > 0, np.frexp(amax)[1] - 1 + 127, 0) - down, 1)
    scale = np.exp2(byte - 127.0)
    codes = (blocks / scale).astype(np.float32).astype(dtype).astype(np.float64)
    return np.moveaxis((codes * scale).reshape(v.shape), -1, axis)


WIDE = False


def mx_kscale(k):
    if not WIDE:
        return np.ones(k)
    levels = np.array([10, -10, 5, -5, 0])
    if k % 512:
        return np.exp2(np.random.permutation(np.resize(levels, k // 32))).repeat(32)
    a = np.empty((k // 512, 16))
    for p in range(k // 512):
        a[p, :8] = np.random.permutation(np.resize(levels, 8))
        for g in range(8):
            far = levels[np.abs(levels - a[p, g]) >= 10]
            a[p, g + 8] = far[np.random.randint(len(far))]
    return np.exp2(a.ravel()).repeat(32)


def f64(x):
    return np.asarray(x).astype(np.float64)


def striped(idx):
    return np.tile(idx.reshape(-1, 16).T, (8, 1)).astype(np.uint16)


def unstriped(offs):
    return offs[:16].T.reshape(-1).astype(np.int64)


def striped8(idx):
    return np.concatenate([x.reshape(-1, 16).T for x in idx]).astype(np.uint16)


def runs(offs, k):
    lists = np.stack([offs[16 * r : 16 * r + 16].T.reshape(-1) for r in range(8)]).astype(np.int64)
    return lists[np.arange(k) % 512 // 64]


def pack_weight(w):
    k, n = w.shape
    w = f64(np.asarray(w, np.float32).astype(ml_dtypes.bfloat16)).reshape(k // 32, 32, n)
    amax = np.abs(w).max(1)
    byte = np.clip(np.where(amax > 0, np.frexp(amax)[1] - 1 + 127 - 7, 1), 1, 254)
    scaled = (w * np.exp2(127.0 - byte)[:, None, :]).reshape(k, n).astype(np.float32)
    words = np.ascontiguousarray(scaled.reshape(k // 512, 128, 4, n).transpose(0, 1, 3, 2)).astype(ml_dtypes.float8_e4m3fn).view(np.uint8)
    return words, np.ascontiguousarray(byte.astype(np.uint8).reshape(k // 512, 16, n))


def unpack_weight(words, scales):
    g, p, n, _ = words.shape
    vals = np.ascontiguousarray(words).view(ml_dtypes.float8_e4m3fn).astype(np.float64) * np.repeat(np.exp2(scales.astype(np.float64) - 127.0), 8, axis=1)[..., None]
    return vals.transpose(0, 1, 3, 2).reshape(g * 512, n)


def relu(v):
    return np.maximum(v, 0.0)


K, T, S, N, H = 512, 2048, 512, 512, 512


def setup_inputs():
    n = np.random.standard_normal
    s = mx_kscale(K)[:, None]
    u = mx_kscale(S)
    packed_xT = pack_weight(n((K, T)) * s)
    return {
        "x_words": packed_xT[0],
        "x_scales": packed_xT[1],
        "wa": (n((K, H)) / np.sqrt(K) / s).astype(np.float32),
        "wb": (n((K, N)) / np.sqrt(K) / s).astype(np.float32),
        "gt": (np.random.uniform(0.5, 1.5, (S, 1)) * u[:, None]).astype(np.float32),
        "gi": (np.random.uniform(0.5, 1.5, (S, 1)) / u[:, None]).astype(np.float32),
        "offs": striped(np.random.permutation(T)[:S]),
        "two": striped(np.random.permutation(T)[:S]),
        "n1": striped8(np.stack([np.random.permutation(H) for _ in range(8)])),
        "n2": striped8(np.stack([np.random.permutation(H) for _ in range(8)])),
        "n3": striped8(np.stack([np.random.permutation(N) for _ in range(8)])),
        "n4": striped8(np.stack([np.random.permutation(N) for _ in range(8)])),
        "n5": striped8(np.stack([np.random.permutation(N) for _ in range(8)])),
        "n6": striped8(np.stack([np.random.permutation(N) for _ in range(8)])),
    }


def reference(x_words, x_scales, wa, wb, gt, gi, offs, two, n1, n2, n3, n4, n5, n6):
    xq = unpack_weight(x_words, x_scales)[:, unstriped(offs)]
    a = xq.T @ mxq(f64(wa), 0, "e4m3")
    z = f64(gt) * ((a[np.arange(S)[:, None], runs(n1, S)]) / (np.abs(a) + np.abs(a[np.arange(S)[:, None], runs(n2, S)]) + 0.5))
    x_two = unpack_weight(x_words, x_scales)[:, unstriped(two)]
    b = x_two.T @ mxq(f64(wb), 0, "e4m3")
    rl = relu(b)
    ds = np.zeros((S, N))
    ds[np.arange(S)[:, None], runs(n3, S)] = rl
    z2 = f64(gi) * (ds - (0.5 * b))
    cv = 0.0625 * ((mxq(z, 0, "e4m3").T @ mxq(z2, 0, "e4m3")))
    return cv + cv[np.arange(H)[:, None], runs(n4, H)] - (np.maximum(cv[np.arange(H)[:, None], runs(n5, H)], cv[np.arange(H)[:, None], runs(n6, H)]))

@@ -1,0 +1,220 @@
+from contextlib import ExitStack
+
+import concourse.mybir as mybir
+from concourse.masks import make_identity
+
+K, T, S, N, H = 512, 2048, 512, 512, 512
+FLOPS = 2 * K * S * H + 2 * K * S * N + 2 * S * H * N
+
+F32 = mybir.dt.float32
+BF16 = mybir.dt.bfloat16
+I32 = mybir.dt.int32
+U32 = mybir.dt.uint32
+U16 = mybir.dt.uint16
+U8 = mybir.dt.uint8
+FP8X4 = mybir.dt.float8_e4m3fn_x4
+ALU = mybir.AluOpType
+ACT = mybir.ActivationFunctionType
+
+P = 128
+PACK = 4
+W = 512
+HALF = W // 2
+RUN = 8
+
+
+def tile_picked_mombnorm2sendtrim_none_p_kernel(
+    tc, x_words, x_scales, wa, wb, gt, gi, offs, two, n1, n2, n3, n4, n5, n6, out
+):
+    nc = tc.nc
+    with ExitStack() as ctx:
+        keep = ctx.enter_context(tc.tile_pool(name="keep", bufs=1))
+        psum = ctx.enter_context(tc.psum_pool(name="psum", bufs=1))
+
+        def load_list(name, src):
+            lst = keep.tile([P, W // 16], U16, name=name)
+            nc.sync.dma_start(lst[:], src)
+            return lst
+
+        def load_weight_half(name, w, h, tag):
+            raw = keep.tile([P, PACK, HALF], F32, name=name, tag=tag, align_bytes=64)
+            nc.sync.dma_start(raw[:], w.rearrange("(p j) c -> p j c", j=PACK)[:, :, h * HALF : (h + 1) * HALF])
+            return raw
+
+        half_col = keep.tile([P, 1], F32, name="half_col")
+        nc.gpsimd.memset(half_col[:], 0.5)
+        warm = keep.tile([P, 1], F32, name="warm")
+        nc.scalar.activation(warm[:], half_col[:], ACT.Ln)
+        xs = keep.tile([P, T], U8, name="xs", tag="xs", align_bytes=64)
+        nc.vector.memset(xs[:].bitcast(I32), 0)
+        l_two = load_list("l_two", two)
+        l_offs = load_list("l_offs", offs)
+        for q in range(4):
+            nc.sync.dma_start(xs[32 * q : 32 * q + 4, :].bitcast(I32), x_scales[0, 4 * q : 4 * q + 4, :].bitcast(I32))
+        wb_raw = keep.tile([P, PACK, W], F32, name="wb_raw")
+        nc.sync.dma_start(wb_raw[:], wb.rearrange("(p j) c -> p j c", j=PACK))
+        xw = keep.tile([P, T], I32, name="xw")
+        nc.sync.dma_start(xw[:], x_words[0].rearrange("p n t -> p (n t)").bitcast(I32))
+        l3 = load_list("l3", n3)
+        l2 = load_list("l2", n2)
+        l1 = load_list("l1", n1)
+        l5 = load_list("l5", n5)
+        l6 = load_list("l6", n6)
+        l4 = load_list("l4", n4)
+        gain_rows = keep.tile([P, P], F32, name="gain_rows")
+        nc.gpsimd.memset(gain_rows[:], 0.0)
+        for first, g in ((0, gt), (PACK, gi)):
+            nc.gpsimd.dma_start(
+                gain_rows[first : first + PACK, :].rearrange("t (b c) -> t b c", c=RUN),
+                g.rearrange("(b t c) o -> t b (c o)", t=PACK, c=RUN),
+            )
+        ident = keep.tile([P, P], F32, name="ident")
+        make_identity(nc, ident[:])
+
+        def pick_scales(name, lst):
+            picked = keep.tile([P, W], U8, name=name + "_sp", tag=name + "_sp", align_bytes=64)
+            nc.vector.tensor_copy(picked[:], xs[:].indirect(lst[:]))
+            dealt = keep.tile([P, W], U8, name=name + "_s", align_bytes=64)
+            nc.vector.tensor_copy(
+                dealt[:].bitcast(I32).rearrange("p (t b e) -> p t b e", t=PACK, e=RUN // 4),
+                picked[:].bitcast(I32).rearrange("p (b t e) -> p t b e", t=PACK, e=RUN // 4),
+            )
+            return dealt
+
+        def pick_words(name, lst, tag):
+            dealt = keep.tile([P, W], U32, name=name + "_w", tag=tag, align_bytes=64)
+            nc.vector.tensor_copy(
+                dealt[:].rearrange("p (t b c) -> p b t c", t=PACK, c=RUN), xw[:].bitcast(U32).indirect(lst[:])
+            )
+            return dealt
+
+        def cast_weight(name, raw):
+            grouped = keep.tile([P, W, PACK], BF16, name=name + "_bf", tag="xb_w", align_bytes=64)
+            for h in range(2):
+                nc.scalar.copy(grouped[:, h * HALF : (h + 1) * HALF, :], raw[h][:].rearrange("p j c -> p c j"))
+            return grouped
+
+        def quantize(name, grouped, width):
+            codes = keep.tile([P, width], U32, name=name + "_q", align_bytes=64)
+            scales = keep.tile([P, width], U8, name=name + "_qs", align_bytes=64)
+            nc.vector.quantize_mx(out=codes[:].bitcast(FP8X4), scales=scales[:], in_=grouped[:].rearrange("p c j -> p (c j)"))
+            return codes, scales
+
+        def product(tag, lhs, lhs_s, rhs, rhs_s):
+            bank = psum.tile([P, W], F32, name=tag, tag=tag)
+            nc.tensor.matmul_mx(
+                out=bank[:], lhsT=lhs.bitcast(FP8X4), lhsT_scale=lhs_s, rhs=rhs.bitcast(FP8X4), rhs_scale=rhs_s,
+                start=True, stop=True,
+            )
+            return bank
+
+        xb_s = pick_scales("xb", l_two)
+        xa_s = pick_scales("xa", l_offs)
+        wa_raw = [load_weight_half("wa_raw%d" % h, wa, h, ("xb_sp", "xs")[h]) for h in range(2)]
+        wb_bf = keep.tile([P, W, PACK], BF16, name="wb_bf", tag="wb_bf", align_bytes=64)
+        wb_view = wb_raw[:].rearrange("p j c -> p c j")
+        nc.scalar.copy(wb_bf[:, 0:HALF, :], wb_view[:, 0:HALF, :])
+        nc.vector.tensor_copy(wb_bf[:, HALF:W, :], wb_view[:, HALF:W, :])
+        wb_q, wb_s = quantize("wb", wb_bf, W)
+        xb_w = pick_words("xb", l_two, "xb_w")
+        xa_w = pick_words("xa", l_offs, "xa_w")
+        gains = psum.tile([P, W], F32, name="gains", tag="a0")
+        nc.tensor.transpose(gains[:, 0:P], gain_rows[:], ident[:])
+        gt_sb, gi_sb = gains[:, 0:PACK], gains[:, PACK : 2 * PACK]
+
+        gi_abs = keep.tile([P, PACK], F32, name="gi_abs")
+        nc.scalar.activation(gi_abs[:], gi_sb, ACT.Abs)
+        gi_half = keep.tile([P, PACK], F32, name="gi_half")
+        nc.scalar.activation(gi_half[:], gi_sb, ACT.Abs, scale=0.5)
+        sign2 = keep.tile([P, PACK], F32, name="sign2")
+        nc.vector.tensor_scalar(sign2[:], gi_sb, 0.0, 2.0, ALU.is_ge, ALU.mult)
+        gt_signed = keep.tile([P, PACK], F32, name="gt_signed")
+        nc.vector.scalar_tensor_tensor(gt_signed[:], sign2[:], -1.0, gt_sb, ALU.add, ALU.mult)
+
+        cols = [slice(t * P, (t + 1) * P) for t in range(PACK)]
+        b_bank = [product("b%d" % t, xb_w[:, cols[t]], xb_s[:, cols[t]], wb_q[:], wb_s[:]) for t in range(PACK)]
+
+        a_abs = [keep.tile([P, 2 * W], F32, name="a_abs%d" % t) for t in range(PACK)]
+        a_num = [keep.tile([P, 2 * W], F32, name="a_num%d" % t) for t in range(PACK)]
+        ds = [keep.tile([P, 2 * W], F32, name="ds%d" % t) for t in range(2)]
+        ds = ds + [a_abs[3], keep.tile([P, 2 * W], F32, name="ds3")]
+
+        def send(t, tag):
+            rl = keep.tile([P, W], F32, name="rl%d" % t, tag=tag, align_bytes=64)
+            nc.scalar.activation(rl[:], b_bank[t][:], ACT.Relu, scale=gi_abs[:, t : t + 1])
+            nc.vector.tensor_copy(ds[t][:].indirect(l3[:]), rl[:])
+
+        send(0, "rl0")
+        wa_bf = cast_weight("wa", wa_raw)
+        wa_q, wa_s = quantize("wa", wa_bf, W)
+        send(1, "xs")
+        a_bank = [product("a%d" % t, xa_w[:, cols[t]], xa_s[:, cols[t]], wa_q[:], wa_s[:]) for t in range(PACK)]
+        den = keep.tile([P, PACK, W], F32, name="den")
+        for t in range(PACK):
+            nc.scalar.activation(a_abs[t][:, 0:W], a_bank[t][:], ACT.Abs)
+            own = keep.tile([P, W], F32, name="own%d" % t, tag="own%d" % t)
+            nc.scalar.activation(own[:], a_bank[t][:], ACT.Abs)
+            nc.vector.tensor_tensor(den[:, t, :], a_abs[t][:].indirect(l2[:]), own[:], ALU.add)
+        send(2, "rl2")
+        for t in range(PACK):
+            nc.scalar.activation(a_num[t][:, 0:W], a_bank[t][:], ACT.Copy, scale=gt_signed[:, t : t + 1])
+        log_den = keep.tile([P, PACK, W], F32, name="log_den")
+        nc.scalar.activation(log_den[:], den[:], ACT.Ln, bias=half_col[:])
+        z2_bf = keep.tile([P, PACK, W], BF16, name="z2_bf", tag="own3")
+
+        def finish_z2(t):
+            nc.vector.scalar_tensor_tensor(
+                z2_bf[:, t, :], b_bank[t][:], gi_half[:, t : t + 1], ds[t][:, 0:W], ALU.mult, ALU.subtract
+            )
+
+        finish_z2(0)
+        finish_z2(1)
+        send(3, "rl2")
+        rec = keep.tile([P, PACK, W], F32, name="rec")
+        nc.scalar.activation(rec[:], log_den[:], ACT.Exp, scale=-1.0)
+        finish_z2(2)
+        finish_z2(3)
+        z2_grouped = keep.tile([P, W, PACK], BF16, name="z2_grouped", align_bytes=64)
+        nc.scalar.copy(z2_grouped[:], z2_bf[:].rearrange("p t c -> p c t"))
+        z = [keep.tile([P, PACK, HALF], F32, name="z%d" % h) for h in range(2)]
+        z_grouped = [keep.tile([P, P, PACK], BF16, name="z_grouped%d" % u, align_bytes=64) for u in range(PACK)]
+        for h in range(2):
+            for t in range(PACK):
+                nc.vector.tensor_tensor(
+                    z[h][:, t, :],
+                    a_num[t][:].indirect(l1[:, h * HALF // 16 : (h + 1) * HALF // 16]),
+                    rec[:, t, h * HALF : (h + 1) * HALF],
+                    ALU.mult,
+                )
+        z_view = [z[h][:].rearrange("p t (m u) -> p u m t", u=PACK) for h in range(2)]
+        for u in range(PACK):
+            nc.scalar.copy(z_grouped[u][:, 0 : P // 2, :], z_view[0][:, u])
+        z2_q, z2_s = quantize("z2", z2_grouped, W)
+
+        out_rows = out.rearrange("(p u) c -> p u c", u=PACK)
+        win, plain = a_num, []
+
+        def group_late(u):
+            nc.vector.tensor_copy(z_grouped[u][:, P // 2 : P, :], z_view[1][:, u])
+
+        group_late(0)
+        for u in range(PACK):
+            if u + 1 < PACK:
+                group_late(u + 1)
+            z_q, z_s = quantize("zu%d" % u, z_grouped[u], P)
+            bank = product("a%d" % u, z_q[:], z_s[:], z2_q[:], z2_s[:])
+            nc.scalar.activation(a_num[u][:, 0:W], bank[:], ACT.Copy, scale=-0.0625)
+            cv = keep.tile([P, W], F32, name="cv%d" % u)
+            nc.scalar.activation(cv[:], bank[:], ACT.Copy, scale=-0.0625)
+            plain.append(cv)
+        d5 = keep.tile([P, PACK, W], F32, name="d5")
+        d6 = keep.tile([P, PACK, W], F32, name="d6")
+        for u in range(PACK):
+            nc.vector.tensor_tensor(d5[:, u, :], win[u][:].indirect(l5[:]), plain[u][:], ALU.subtract)
+            nc.vector.tensor_tensor(d6[:, u, :], win[u][:].indirect(l6[:]), plain[u][:], ALU.subtract)
+        big = keep.tile([P, PACK, W], F32, name="big")
+        nc.vector.tensor_tensor(big[:], d5[:], d6[:], ALU.max)
+        for u in range(PACK):
+            res = keep.tile([P, W], F32, name="res%d" % u)
+            nc.vector.tensor_tensor(res[:], win[u][:].indirect(l4[:]), big[:, u, :], ALU.subtract)
+            nc.sync.dma_start(out_rows[:, u, :], res[:])

@@ -41,8 +41,17 @@ def tile_picked_mombnorm2sendtrim_none_p_kernel(
             nc.sync.dma_start(raw[:], w.rearrange("(p j) c -> p j c", j=PACK)[:, :, h * HALF : (h + 1) * HALF])
             return raw
 
+        gain_rows = []
+        for name, g in (("gi_rows", gi), ("gt_rows", gt)):
+            rows = keep.tile([P, P], F32, name=name)
+            nc.gpsimd.memset(rows[:], 0.0)
+            nc.gpsimd.dma_start(
+                rows[0:PACK, :].rearrange("t (b c) -> t b c", c=RUN),
+                g.rearrange("(b t c) o -> t b (c o)", t=PACK, c=RUN),
+            )
+            gain_rows.append(rows)
         half_col = keep.tile([P, 1], F32, name="half_col")
-        nc.gpsimd.memset(half_col[:], 0.5)
+        nc.vector.memset(half_col[:], 0.5)
         warm = keep.tile([P, 1], F32, name="warm")
         nc.scalar.activation(warm[:], half_col[:], ACT.Ln)
         xs = keep.tile([P, T], U8, name="xs", tag="xs", align_bytes=64)
@@ -51,23 +60,15 @@ def tile_picked_mombnorm2sendtrim_none_p_kernel(
         l_offs = load_list("l_offs", offs)
         for q in range(4):
             nc.sync.dma_start(xs[32 * q : 32 * q + 4, :].bitcast(I32), x_scales[0, 4 * q : 4 * q + 4, :].bitcast(I32))
-        wb_raw = keep.tile([P, PACK, W], F32, name="wb_raw")
-        nc.sync.dma_start(wb_raw[:], wb.rearrange("(p j) c -> p j c", j=PACK))
         xw = keep.tile([P, T], I32, name="xw")
         nc.sync.dma_start(xw[:], x_words[0].rearrange("p n t -> p (n t)").bitcast(I32))
+        wb_raw = [load_weight_half("wb_raw%d" % h, wb, h, "wb_raw%d" % h) for h in range(2)]
         l3 = load_list("l3", n3)
         l2 = load_list("l2", n2)
         l1 = load_list("l1", n1)
         l5 = load_list("l5", n5)
         l6 = load_list("l6", n6)
         l4 = load_list("l4", n4)
-        gain_rows = keep.tile([P, P], F32, name="gain_rows")
-        nc.gpsimd.memset(gain_rows[:], 0.0)
-        for first, g in ((0, gt), (PACK, gi)):
-            nc.gpsimd.dma_start(
-                gain_rows[first : first + PACK, :].rearrange("t (b c) -> t b c", c=RUN),
-                g.rearrange("(b t c) o -> t b (c o)", t=PACK, c=RUN),
-            )
         ident = keep.tile([P, P], F32, name="ident")
         make_identity(nc, ident[:])
 
@@ -100,39 +101,50 @@ def tile_picked_mombnorm2sendtrim_none_p_kernel(
             nc.vector.quantize_mx(out=codes[:].bitcast(FP8X4), scales=scales[:], in_=grouped[:].rearrange("p c j -> p (c j)"))
             return codes, scales
 
-        def product(tag, lhs, lhs_s, rhs, rhs_s):
-            bank = psum.tile([P, W], F32, name=tag, tag=tag)
+        def multiply(dst, lhs, lhs_s, rhs, rhs_s):
             nc.tensor.matmul_mx(
-                out=bank[:], lhsT=lhs.bitcast(FP8X4), lhsT_scale=lhs_s, rhs=rhs.bitcast(FP8X4), rhs_scale=rhs_s,
+                out=dst, lhsT=lhs.bitcast(FP8X4), lhsT_scale=lhs_s, rhs=rhs.bitcast(FP8X4), rhs_scale=rhs_s,
                 start=True, stop=True,
             )
+
+        def product(tag, lhs, lhs_s, rhs, rhs_s):
+            bank = psum.tile([P, W], F32, name=tag, tag=tag)
+            multiply(bank[:], lhs, lhs_s, rhs, rhs_s)
             return bank
 
         xb_s = pick_scales("xb", l_two)
         xa_s = pick_scales("xa", l_offs)
         wa_raw = [load_weight_half("wa_raw%d" % h, wa, h, ("xb_sp", "xs")[h]) for h in range(2)]
-        wb_bf = keep.tile([P, W, PACK], BF16, name="wb_bf", tag="wb_bf", align_bytes=64)
-        wb_view = wb_raw[:].rearrange("p j c -> p c j")
-        nc.scalar.copy(wb_bf[:, 0:HALF, :], wb_view[:, 0:HALF, :])
-        nc.vector.tensor_copy(wb_bf[:, HALF:W, :], wb_view[:, HALF:W, :])
-        wb_q, wb_s = quantize("wb", wb_bf, W)
         xb_w = pick_words("xb", l_two, "xb_w")
         xa_w = pick_words("xa", l_offs, "xa_w")
-        gains = psum.tile([P, W], F32, name="gains", tag="a0")
-        nc.tensor.transpose(gains[:, 0:P], gain_rows[:], ident[:])
-        gt_sb, gi_sb = gains[:, 0:PACK], gains[:, PACK : 2 * PACK]
+        halves = [slice(h * HALF, (h + 1) * HALF) for h in range(2)]
+        wb_q = keep.tile([P, W], U32, name="wb_q", align_bytes=64)
+        wb_s = keep.tile([P, W], U8, name="wb_qs", align_bytes=64)
+        for h, cast in enumerate((nc.scalar.copy, nc.vector.tensor_copy)):
+            wb_bf = keep.tile([P, HALF, PACK], BF16, name="wb_bf%d" % h, align_bytes=64)
+            cast(wb_bf[:], wb_raw[h][:].rearrange("p j c -> p c j"))
+            nc.vector.quantize_mx(
+                out=wb_q[:, halves[h]].bitcast(FP8X4), scales=wb_s[:, halves[h]], in_=wb_bf[:].rearrange("p c j -> p (c j)")
+            )
+        gains = [psum.tile([P, P], F32, name="gains%d" % i, tag="a%d" % i) for i in range(2)]
+        for i in range(2):
+            nc.tensor.transpose(gains[i][:], gain_rows[i][:], ident[:])
+        gi_sb, gt_sb = gains[0][:, 0:PACK], gains[1][:, 0:PACK]
 
         gi_abs = keep.tile([P, PACK], F32, name="gi_abs")
         nc.scalar.activation(gi_abs[:], gi_sb, ACT.Abs)
         gi_half = keep.tile([P, PACK], F32, name="gi_half")
         nc.scalar.activation(gi_half[:], gi_sb, ACT.Abs, scale=0.5)
-        sign2 = keep.tile([P, PACK], F32, name="sign2")
-        nc.vector.tensor_scalar(sign2[:], gi_sb, 0.0, 2.0, ALU.is_ge, ALU.mult)
+        gi_sign = keep.tile([P, PACK], F32, name="gi_sign")
+        nc.scalar.activation(gi_sign[:], gi_sb, ACT.Sign)
+        gi_unit = keep.tile([P, PACK], F32, name="gi_unit")
+        nc.scalar.activation(gi_unit[:], gi_sign[:], ACT.Sign, bias=half_col[:])
         gt_signed = keep.tile([P, PACK], F32, name="gt_signed")
-        nc.vector.scalar_tensor_tensor(gt_signed[:], sign2[:], -1.0, gt_sb, ALU.add, ALU.mult)
+        for t in range(PACK):
+            nc.scalar.activation(gt_signed[:, t : t + 1], gt_sb[:, t : t + 1], ACT.Copy, scale=gi_unit[:, t : t + 1])
 
         cols = [slice(t * P, (t + 1) * P) for t in range(PACK)]
-        b_bank = [product("b%d" % t, xb_w[:, cols[t]], xb_s[:, cols[t]], wb_q[:], wb_s[:]) for t in range(PACK)]
+        b_bank = [psum.tile([P, W], F32, name="b%d" % t, tag="b%d" % t) for t in range(PACK)]
 
         a_abs = [keep.tile([P, 2 * W], F32, name="a_abs%d" % t) for t in range(PACK)]
         a_num = [keep.tile([P, 2 * W], F32, name="a_num%d" % t) for t in range(PACK)]
@@ -144,7 +156,14 @@ def tile_picked_mombnorm2sendtrim_none_p_kernel(
             nc.scalar.activation(rl[:], b_bank[t][:], ACT.Relu, scale=gi_abs[:, t : t + 1])
             nc.vector.tensor_copy(ds[t][:].indirect(l3[:]), rl[:])
 
-        send(0, "rl0")
+        lanes = [slice(h * HALF // 16, (h + 1) * HALF // 16) for h in range(2)]
+        for h in range(2):
+            multiply(b_bank[0][:, halves[h]], xb_w[:, cols[0]], xb_s[:, cols[0]], wb_q[:, halves[h]], wb_s[:, halves[h]])
+            rl = keep.tile([P, HALF], F32, name="rl0_%d" % h)
+            nc.scalar.activation(rl[:], b_bank[0][:, halves[h]], ACT.Relu, scale=gi_abs[:, 0:1])
+            nc.vector.tensor_copy(ds[0][:].indirect(l3[:, lanes[h]]), rl[:])
+        for t in range(1, PACK):
+            multiply(b_bank[t][:], xb_w[:, cols[t]], xb_s[:, cols[t]], wb_q[:], wb_s[:])
         wa_bf = cast_weight("wa", wa_raw)
         wa_q, wa_s = quantize("wa", wa_bf, W)
         send(1, "xs")
@@ -192,7 +211,8 @@ def tile_picked_mombnorm2sendtrim_none_p_kernel(
         z2_q, z2_s = quantize("z2", z2_grouped, W)
 
         out_rows = out.rearrange("(p u) c -> p u c", u=PACK)
-        win, plain = a_num, []
+        win, banks = a_num, []
+        turned_tiles = 2
 
         def group_late(u):
             nc.vector.tensor_copy(z_grouped[u][:, P // 2 : P, :], z_view[1][:, u])
@@ -203,18 +223,60 @@ def tile_picked_mombnorm2sendtrim_none_p_kernel(
                 group_late(u + 1)
             z_q, z_s = quantize("zu%d" % u, z_grouped[u], P)
             bank = product("a%d" % u, z_q[:], z_s[:], z2_q[:], z2_s[:])
-            nc.scalar.activation(a_num[u][:, 0:W], bank[:], ACT.Copy, scale=-0.0625)
-            cv = keep.tile([P, W], F32, name="cv%d" % u)
-            nc.scalar.activation(cv[:], bank[:], ACT.Copy, scale=-0.0625)
-            plain.append(cv)
-        d5 = keep.tile([P, PACK, W], F32, name="d5")
-        d6 = keep.tile([P, PACK, W], F32, name="d6")
-        for u in range(PACK):
-            nc.vector.tensor_tensor(d5[:, u, :], win[u][:].indirect(l5[:]), plain[u][:], ALU.subtract)
-            nc.vector.tensor_tensor(d6[:, u, :], win[u][:].indirect(l6[:]), plain[u][:], ALU.subtract)
-        big = keep.tile([P, PACK, W], F32, name="big")
-        nc.vector.tensor_tensor(big[:], d5[:], d6[:], ALU.max)
-        for u in range(PACK):
-            res = keep.tile([P, W], F32, name="res%d" % u)
-            nc.vector.tensor_tensor(res[:], win[u][:].indirect(l4[:]), big[:, u, :], ALU.subtract)
-            nc.sync.dma_start(out_rows[:, u, :], res[:])
+            nc.scalar.activation(win[u][:, 0:W], bank[:], ACT.Copy, scale=-0.0625)
+            banks.append(bank)
+
+        direct = range(turned_tiles, PACK)
+        cv = keep.tile([P, len(direct), W], F32, name="cv")
+        for i, u in enumerate(direct):
+            nc.scalar.activation(cv[:, i, :], banks[u][:], ACT.Copy, scale=-0.0625)
+        g5 = [keep.tile([P, W], F32, name="g5_%d" % u) for u in range(turned_tiles)]
+        rest = keep.tile([P, PACK, W], F32, name="rest")
+
+        def fetch5(u):
+            nc.vector.tensor_copy(g5[u][:], win[u][:].indirect(l5[:]))
+
+        def rest_on_tensor(u):
+            d65 = keep.tile([P, W], F32, name="d65_%d" % u)
+            nc.vector.tensor_tensor(d65[:], win[u][:].indirect(l6[:]), g5[u][:], ALU.subtract)
+            minus_cv = keep.tile([P, W], F32, name="minus_cv%d" % u)
+            nc.scalar.activation(minus_cv[:], banks[u][:], ACT.Copy, scale=0.0625)
+            excess = keep.tile([P, W], F32, name="excess%d" % u)
+            nc.scalar.activation(excess[:], d65[:], ACT.Relu)
+            turned = psum.tile([P, W], F32, name="turned%d" % u, tag="b%d" % (u % 2))
+            terms = (minus_cv, g5[u], excess)
+            for k in range(PACK):
+                for i, term in enumerate(terms):
+                    nc.tensor.matmul(
+                        turned[:, cols[k]], term[:, cols[k]], ident[:], start=i == 0, stop=i == len(terms) - 1,
+                        is_transpose=True,
+                    )
+            turned_sb = keep.tile([P, W], F32, name="turned_sb%d" % u)
+            nc.scalar.copy(turned_sb[:], turned[:])
+            back = psum.tile([P, W], F32, name="back%d" % u, tag="b%d" % (2 + u % 2))
+            for k in range(PACK):
+                nc.tensor.transpose(back[:, cols[k]], turned_sb[:, cols[k]], ident[:])
+            nc.scalar.copy(rest[:, u, :], back[:])
+
+        for u in range(turned_tiles):
+            fetch5(u)
+        for u in range(turned_tiles):
+            rest_on_tensor(u)
+
+        d5 = keep.tile([P, len(direct), W], F32, name="d5")
+        d6 = keep.tile([P, len(direct), W], F32, name="d6")
+        for i, u in enumerate(direct):
+            nc.vector.tensor_tensor(d5[:, i, :], win[u][:].indirect(l5[:]), cv[:, i, :], ALU.subtract)
+            nc.vector.tensor_tensor(d6[:, i, :], win[u][:].indirect(l6[:]), cv[:, i, :], ALU.subtract)
+        nc.vector.tensor_tensor(rest[:, turned_tiles:PACK, :], d5[:], d6[:], ALU.max)
+        for u in (0, 2, 3, 1):
+            pieces = 2 if u == 1 else 1
+            width = W // pieces
+            for h in range(pieces):
+                span = slice(h * width, (h + 1) * width)
+                res = keep.tile([P, width], F32, name="res%d_%d" % (u, h))
+                nc.vector.tensor_tensor(
+                    res[:], win[u][:].indirect(l4[:, h * width // 16 : (h + 1) * width // 16]), rest[:, u, span],
+                    ALU.subtract,
+                )
+                nc.sync.dma_start(out_rows[:, u, span], res[:])

@@ -89,10 +89,13 @@ def tile_picked_mombnorm2sendtrim_none_p_kernel(
             )
             return dealt
 
+        def interleave(copy, grouped, planes):
+            copy(grouped.rearrange("p (c i) j -> p c j i", i=PACK), planes.rearrange("p j (c i) -> p c j i", i=PACK))
+
         def cast_weight(name, raw):
             grouped = keep.tile([P, W, PACK], BF16, name=name + "_bf", tag="xb_w", align_bytes=64)
             for h in range(2):
-                nc.scalar.copy(grouped[:, h * HALF : (h + 1) * HALF, :], raw[h][:].rearrange("p j c -> p c j"))
+                interleave(nc.scalar.copy, grouped[:, h * HALF : (h + 1) * HALF, :], raw[h][:])
             return grouped
 
         def quantize(name, grouped, width):
@@ -122,7 +125,7 @@ def tile_picked_mombnorm2sendtrim_none_p_kernel(
         wb_s = keep.tile([P, W], U8, name="wb_qs", align_bytes=64)
         for h, cast in enumerate((nc.scalar.copy, nc.vector.tensor_copy)):
             wb_bf = keep.tile([P, HALF, PACK], BF16, name="wb_bf%d" % h, align_bytes=64)
-            cast(wb_bf[:], wb_raw[h][:].rearrange("p j c -> p c j"))
+            interleave(cast, wb_bf[:], wb_raw[h][:])
             nc.vector.quantize_mx(
                 out=wb_q[:, halves[h]].bitcast(FP8X4), scales=wb_s[:, halves[h]], in_=wb_bf[:].rearrange("p c j -> p (c j)")
             )
@@ -194,35 +197,39 @@ def tile_picked_mombnorm2sendtrim_none_p_kernel(
         finish_z2(2)
         finish_z2(3)
         z2_grouped = keep.tile([P, W, PACK], BF16, name="z2_grouped", align_bytes=64)
-        nc.scalar.copy(z2_grouped[:], z2_bf[:].rearrange("p t c -> p c t"))
-        z = [keep.tile([P, PACK, HALF], F32, name="z%d" % h) for h in range(2)]
-        z_grouped = [keep.tile([P, P, PACK], BF16, name="z_grouped%d" % u, align_bytes=64) for u in range(PACK)]
-        for h in range(2):
+        interleave(nc.scalar.copy, z2_grouped[:], z2_bf[:])
+        z_grouped = keep.tile([P, PACK, P, PACK], BF16, name="z_grouped", align_bytes=64)
+        early = 3 * W // 4
+        parts = []
+        for c0, c1 in ((0, early), (early, W)):
+            z = keep.tile([P, PACK, c1 - c0], F32, name="z%d" % c0)
             for t in range(PACK):
                 nc.vector.tensor_tensor(
-                    z[h][:, t, :],
-                    a_num[t][:].indirect(l1[:, h * HALF // 16 : (h + 1) * HALF // 16]),
-                    rec[:, t, h * HALF : (h + 1) * HALF],
-                    ALU.mult,
+                    z[:, t, :], a_num[t][:].indirect(l1[:, c0 // 16 : c1 // 16]), rec[:, t, c0:c1], ALU.mult
                 )
-        z_view = [z[h][:].rearrange("p t (m u) -> p u m t", u=PACK) for h in range(2)]
-        for u in range(PACK):
-            nc.scalar.copy(z_grouped[u][:, 0 : P // 2, :], z_view[0][:, u])
+            parts.append(
+                (
+                    z_grouped[:, :, c0 // PACK : c1 // PACK, :].rearrange("p u m t -> p m t u"),
+                    z[:].rearrange("p t (m u) -> p m t u", u=PACK),
+                )
+            )
+        nc.scalar.copy(*parts[0])
         z2_q, z2_s = quantize("z2", z2_grouped, W)
+        nc.vector.tensor_copy(*parts[1])
 
         out_rows = out.rearrange("(p u) c -> p u c", u=PACK)
         win, banks = a_num, []
         turned_tiles = 2
-
-        def group_late(u):
-            nc.vector.tensor_copy(z_grouped[u][:, P // 2 : P, :], z_view[1][:, u])
-
-        group_late(0)
+        z_q = keep.tile([P, W], U32, name="z_q", align_bytes=64)
+        z_s = keep.tile([P, W], U8, name="z_s", align_bytes=64)
+        for u0, u1 in ((0, 1), (1, 2), (2, 4)):
+            nc.vector.quantize_mx(
+                out=z_q[:, u0 * P : u1 * P].bitcast(FP8X4),
+                scales=z_s[:, u0 * P : u1 * P],
+                in_=z_grouped[:, u0:u1].rearrange("p u m t -> p (u m t)"),
+            )
         for u in range(PACK):
-            if u + 1 < PACK:
-                group_late(u + 1)
-            z_q, z_s = quantize("zu%d" % u, z_grouped[u], P)
-            bank = product("a%d" % u, z_q[:], z_s[:], z2_q[:], z2_s[:])
+            bank = product("a%d" % u, z_q[:, cols[u]], z_s[:, cols[u]], z2_q[:], z2_s[:])
             nc.scalar.activation(win[u][:, 0:W], bank[:], ACT.Copy, scale=-0.0625)
             banks.append(bank)
 
@@ -269,7 +276,7 @@ def tile_picked_mombnorm2sendtrim_none_p_kernel(
             nc.vector.tensor_tensor(d5[:, i, :], win[u][:].indirect(l5[:]), cv[:, i, :], ALU.subtract)
             nc.vector.tensor_tensor(d6[:, i, :], win[u][:].indirect(l6[:]), cv[:, i, :], ALU.subtract)
         nc.vector.tensor_tensor(rest[:, turned_tiles:PACK, :], d5[:], d6[:], ALU.max)
-        for u in (0, 2, 3, 1):
+        for u in (2, 3, 0, 1):
             pieces = 2 if u == 1 else 1
             width = W // pieces
             for h in range(pieces):

@@ -36,20 +36,20 @@ def tile_picked_mombnorm2sendtrim_none_p_kernel(
             nc.sync.dma_start(lst[:], src)
             return lst
 
-        def load_weight_half(name, w, h, tag):
-            raw = keep.tile([P, PACK, HALF], F32, name=name, tag=tag, align_bytes=64)
-            nc.sync.dma_start(raw[:], w.rearrange("(p j) c -> p j c", j=PACK)[:, :, h * HALF : (h + 1) * HALF])
+        def load_weight_part(name, w, c0, c1, tag):
+            raw = keep.tile([P, PACK, c1 - c0], F32, name=name, tag=tag, align_bytes=64)
+            nc.sync.dma_start(raw[:], w.rearrange("(p j) c -> p j c", j=PACK)[:, :, c0:c1])
             return raw
 
-        gain_rows = []
-        for name, g in (("gi_rows", gi), ("gt_rows", gt)):
+        def load_gain(name, g):
             rows = keep.tile([P, P], F32, name=name)
             nc.gpsimd.memset(rows[:], 0.0)
-            nc.gpsimd.dma_start(
+            nc.sync.dma_start(
                 rows[0:PACK, :].rearrange("t (b c) -> t b c", c=RUN),
                 g.rearrange("(b t c) o -> t b (c o)", t=PACK, c=RUN),
             )
-            gain_rows.append(rows)
+            return rows
+
         half_col = keep.tile([P, 1], F32, name="half_col")
         nc.vector.memset(half_col[:], 0.5)
         warm = keep.tile([P, 1], F32, name="warm")
@@ -60,10 +60,13 @@ def tile_picked_mombnorm2sendtrim_none_p_kernel(
         l_offs = load_list("l_offs", offs)
         for q in range(4):
             nc.sync.dma_start(xs[32 * q : 32 * q + 4, :].bitcast(I32), x_scales[0, 4 * q : 4 * q + 4, :].bitcast(I32))
+        gi_rows = load_gain("gi_rows", gi)
         xw = keep.tile([P, T], I32, name="xw")
         nc.sync.dma_start(xw[:], x_words[0].rearrange("p n t -> p (n t)").bitcast(I32))
-        wb_raw = [load_weight_half("wb_raw%d" % h, wb, h, "wb_raw%d" % h) for h in range(2)]
         l3 = load_list("l3", n3)
+        wb_parts = ((0, P), (P, HALF), (HALF, W))
+        wb_raw = [load_weight_part("wb_raw%d" % c0, wb, c0, c1, "wb_raw%d" % c0) for c0, c1 in wb_parts]
+        gt_rows = load_gain("gt_rows", gt)
         l2 = load_list("l2", n2)
         l1 = load_list("l1", n1)
         l5 = load_list("l5", n5)
@@ -117,34 +120,26 @@ def tile_picked_mombnorm2sendtrim_none_p_kernel(
 
         xb_s = pick_scales("xb", l_two)
         xa_s = pick_scales("xa", l_offs)
-        wa_raw = [load_weight_half("wa_raw%d" % h, wa, h, ("xb_sp", "xs")[h]) for h in range(2)]
+        wa_raw = [load_weight_part("wa_raw%d" % h, wa, h * HALF, (h + 1) * HALF, ("xb_sp", "xs")[h]) for h in range(2)]
         xb_w = pick_words("xb", l_two, "xb_w")
-        xa_w = pick_words("xa", l_offs, "xa_w")
         halves = [slice(h * HALF, (h + 1) * HALF) for h in range(2)]
         wb_q = keep.tile([P, W], U32, name="wb_q", align_bytes=64)
         wb_s = keep.tile([P, W], U8, name="wb_qs", align_bytes=64)
-        for h, cast in enumerate((nc.scalar.copy, nc.vector.tensor_copy)):
-            wb_bf = keep.tile([P, HALF, PACK], BF16, name="wb_bf%d" % h, align_bytes=64)
-            interleave(cast, wb_bf[:], wb_raw[h][:])
-            nc.vector.quantize_mx(
-                out=wb_q[:, halves[h]].bitcast(FP8X4), scales=wb_s[:, halves[h]], in_=wb_bf[:].rearrange("p c j -> p (c j)")
-            )
-        gains = [psum.tile([P, P], F32, name="gains%d" % i, tag="a%d" % i) for i in range(2)]
-        for i in range(2):
-            nc.tensor.transpose(gains[i][:], gain_rows[i][:], ident[:])
-        gi_sb, gt_sb = gains[0][:, 0:PACK], gains[1][:, 0:PACK]
 
+        def turn_gain(name, rows, tag):
+            turned = psum.tile([P, P], F32, name=name, tag=tag)
+            nc.tensor.transpose(turned[:], rows[:], ident[:])
+            return turned[:, 0:PACK]
+
+        gi_col = turn_gain("gi_col", gi_rows, "a0")
         gi_abs = keep.tile([P, PACK], F32, name="gi_abs")
-        nc.scalar.activation(gi_abs[:], gi_sb, ACT.Abs)
+        nc.scalar.activation(gi_abs[:], gi_col, ACT.Abs)
         gi_half = keep.tile([P, PACK], F32, name="gi_half")
-        nc.scalar.activation(gi_half[:], gi_sb, ACT.Abs, scale=0.5)
+        nc.scalar.activation(gi_half[:], gi_col, ACT.Abs, scale=0.5)
         gi_sign = keep.tile([P, PACK], F32, name="gi_sign")
-        nc.scalar.activation(gi_sign[:], gi_sb, ACT.Sign)
+        nc.scalar.activation(gi_sign[:], gi_col, ACT.Sign)
         gi_unit = keep.tile([P, PACK], F32, name="gi_unit")
         nc.scalar.activation(gi_unit[:], gi_sign[:], ACT.Sign, bias=half_col[:])
-        gt_signed = keep.tile([P, PACK], F32, name="gt_signed")
-        for t in range(PACK):
-            nc.scalar.activation(gt_signed[:, t : t + 1], gt_sb[:, t : t + 1], ACT.Copy, scale=gi_unit[:, t : t + 1])
 
         cols = [slice(t * P, (t + 1) * P) for t in range(PACK)]
         b_bank = [psum.tile([P, W], F32, name="b%d" % t, tag="b%d" % t) for t in range(PACK)]
@@ -152,52 +147,66 @@ def tile_picked_mombnorm2sendtrim_none_p_kernel(
         a_abs = [keep.tile([P, 2 * W], F32, name="a_abs%d" % t) for t in range(PACK)]
         a_num = [keep.tile([P, 2 * W], F32, name="a_num%d" % t) for t in range(PACK)]
         ds = [keep.tile([P, 2 * W], F32, name="ds%d" % t) for t in range(2)]
-        ds = ds + [a_abs[3], keep.tile([P, 2 * W], F32, name="ds3")]
 
-        def send(t, tag):
-            rl = keep.tile([P, W], F32, name="rl%d" % t, tag=tag, align_bytes=64)
-            nc.scalar.activation(rl[:], b_bank[t][:], ACT.Relu, scale=gi_abs[:, t : t + 1])
-            nc.vector.tensor_copy(ds[t][:].indirect(l3[:]), rl[:])
+        def send(t, c0, c1, tag):
+            rl = keep.tile([P, c1 - c0], F32, name="rl%d_%d" % (t, c0), tag=tag, align_bytes=64)
+            nc.scalar.activation(rl[:], b_bank[t][:, c0:c1], ACT.Relu, scale=gi_abs[:, t : t + 1])
+            nc.vector.tensor_copy(ds[t][:].indirect(l3[:, c0 // 16 : c1 // 16]), rl[:])
 
-        lanes = [slice(h * HALF // 16, (h + 1) * HALF // 16) for h in range(2)]
-        for h in range(2):
-            multiply(b_bank[0][:, halves[h]], xb_w[:, cols[0]], xb_s[:, cols[0]], wb_q[:, halves[h]], wb_s[:, halves[h]])
-            rl = keep.tile([P, HALF], F32, name="rl0_%d" % h)
-            nc.scalar.activation(rl[:], b_bank[0][:, halves[h]], ACT.Relu, scale=gi_abs[:, 0:1])
-            nc.vector.tensor_copy(ds[0][:].indirect(l3[:, lanes[h]]), rl[:])
+        for raw, (c0, c1) in zip(wb_raw, wb_parts):
+            wb_bf = keep.tile([P, c1 - c0, PACK], BF16, name="wb_bf%d" % c0, tag="wb_bf%d" % c0, align_bytes=64)
+            interleave(nc.scalar.copy, wb_bf[:], raw[:])
+            nc.vector.quantize_mx(
+                out=wb_q[:, c0:c1].bitcast(FP8X4), scales=wb_s[:, c0:c1], in_=wb_bf[:].rearrange("p c j -> p (c j)")
+            )
+            multiply(b_bank[0][:, c0:c1], xb_w[:, cols[0]], xb_s[:, cols[0]], wb_q[:, c0:c1], wb_s[:, c0:c1])
+            send(0, c0, c1, "rl0_%d" % c0)
+        xa_w = pick_words("xa", l_offs, "wb_bf0")
         for t in range(1, PACK):
             multiply(b_bank[t][:], xb_w[:, cols[t]], xb_s[:, cols[t]], wb_q[:], wb_s[:])
+        send(1, 0, HALF, "rl1")
         wa_bf = cast_weight("wa", wa_raw)
         wa_q, wa_s = quantize("wa", wa_bf, W)
-        send(1, "xs")
+        send(1, HALF, W, "xs")
+        gt_col = turn_gain("gt_col", gt_rows, "a1")
+        gt_signed = keep.tile([P, PACK], F32, name="gt_signed")
+        for t in range(PACK):
+            nc.scalar.activation(gt_signed[:, t : t + 1], gt_col[:, t : t + 1], ACT.Copy, scale=gi_unit[:, t : t + 1])
         a_bank = [product("a%d" % t, xa_w[:, cols[t]], xa_s[:, cols[t]], wa_q[:], wa_s[:]) for t in range(PACK)]
         den = keep.tile([P, PACK, W], F32, name="den")
         for t in range(PACK):
             nc.scalar.activation(a_abs[t][:, 0:W], a_bank[t][:], ACT.Abs)
-            own = keep.tile([P, W], F32, name="own%d" % t, tag="own%d" % t)
+            own = keep.tile([P, W], F32, name="own%d" % t, tag="own%d" % t, align_bytes=64)
             nc.scalar.activation(own[:], a_bank[t][:], ACT.Abs)
             nc.vector.tensor_tensor(den[:, t, :], a_abs[t][:].indirect(l2[:]), own[:], ALU.add)
-        send(2, "rl2")
+        ds.extend([a_abs[3], keep.tile([P, 2 * W], F32, name="ds3", tag="own3", align_bytes=64)])
+        send(2, 0, W, "xb_sp")
+        send(3, 0, W, "xb_w")
         for t in range(PACK):
             nc.scalar.activation(a_num[t][:, 0:W], a_bank[t][:], ACT.Copy, scale=gt_signed[:, t : t + 1])
-        log_den = keep.tile([P, PACK, W], F32, name="log_den")
+        log_den = keep.tile([P, PACK, W], F32, name="log_den", tag="log_den", align_bytes=64)
         nc.scalar.activation(log_den[:], den[:], ACT.Ln, bias=half_col[:])
-        z2_bf = keep.tile([P, PACK, W], BF16, name="z2_bf", tag="own3")
+        z2_bf = keep.tile([P, PACK, W], BF16, name="z2_bf", tag="xb_sp", align_bytes=64)
 
         def finish_z2(t):
             nc.vector.scalar_tensor_tensor(
                 z2_bf[:, t, :], b_bank[t][:], gi_half[:, t : t + 1], ds[t][:, 0:W], ALU.mult, ALU.subtract
             )
 
-        finish_z2(0)
-        finish_z2(1)
-        send(3, "rl2")
         rec = keep.tile([P, PACK, W], F32, name="rec")
         nc.scalar.activation(rec[:], log_den[:], ACT.Exp, scale=-1.0)
-        finish_z2(2)
-        finish_z2(3)
-        z2_grouped = keep.tile([P, W, PACK], BF16, name="z2_grouped", align_bytes=64)
-        interleave(nc.scalar.copy, z2_grouped[:], z2_bf[:])
+        for t in range(PACK):
+            finish_z2(t)
+        z2_grouped = keep.tile([P, W, PACK], BF16, name="z2_grouped", tag="log_den", align_bytes=64)
+        z2_q = keep.tile([P, W], U32, name="z2_q", align_bytes=64)
+        z2_s = keep.tile([P, W], U8, name="z2_s", align_bytes=64)
+        for h in range(2):
+            interleave(nc.scalar.copy, z2_grouped[:, halves[h], :], z2_bf[:, :, halves[h]])
+            nc.vector.quantize_mx(
+                out=z2_q[:, halves[h]].bitcast(FP8X4),
+                scales=z2_s[:, halves[h]],
+                in_=z2_grouped[:, halves[h], :].rearrange("p c j -> p (c j)"),
+            )
         z_grouped = keep.tile([P, PACK, P, PACK], BF16, name="z_grouped", align_bytes=64)
         early = 3 * W // 4
         parts = []
@@ -214,7 +223,6 @@ def tile_picked_mombnorm2sendtrim_none_p_kernel(
                 )
             )
         nc.scalar.copy(*parts[0])
-        z2_q, z2_s = quantize("z2", z2_grouped, W)
         nc.vector.tensor_copy(*parts[1])
 
         out_rows = out.rearrange("(p u) c -> p u c", u=PACK)

from contextlib import ExitStack

import concourse.mybir as mybir
from concourse.masks import make_identity

K, T, S, N, H = 512, 2048, 512, 512, 512
FLOPS = 2 * K * S * H + 2 * K * S * N + 2 * S * H * N

F32 = mybir.dt.float32
BF16 = mybir.dt.bfloat16
I32 = mybir.dt.int32
U32 = mybir.dt.uint32
U16 = mybir.dt.uint16
U8 = mybir.dt.uint8
FP8X4 = mybir.dt.float8_e4m3fn_x4
ALU = mybir.AluOpType
ACT = mybir.ActivationFunctionType

P = 128
PACK = 4
W = 512
HALF = W // 2
RUN = 8


def tile_picked_mombnorm2sendtrim_none_p_kernel(
    tc, x_words, x_scales, wa, wb, gt, gi, offs, two, n1, n2, n3, n4, n5, n6, out
):
    nc = tc.nc
    with ExitStack() as ctx:
        keep = ctx.enter_context(tc.tile_pool(name="keep", bufs=1))
        psum = ctx.enter_context(tc.psum_pool(name="psum", bufs=1))

        def load_list(name, src):
            lst = keep.tile([P, W // 16], U16, name=name)
            nc.sync.dma_start(lst[:], src)
            return lst

        def load_weight_part(name, w, c0, c1, tag):
            raw = keep.tile([P, PACK, c1 - c0], F32, name=name, tag=tag, align_bytes=64)
            nc.sync.dma_start(raw[:], w.rearrange("(p j) c -> p j c", j=PACK)[:, :, c0:c1])
            return raw

        def load_gain(name, g):
            rows = keep.tile([P, P], F32, name=name)
            nc.gpsimd.memset(rows[:], 0.0)
            nc.sync.dma_start(
                rows[0:PACK, :].rearrange("t (b c) -> t b c", c=RUN),
                g.rearrange("(b t c) o -> t b (c o)", t=PACK, c=RUN),
            )
            return rows

        half_col = keep.tile([P, 1], F32, name="half_col")
        nc.vector.memset(half_col[:], 0.5)
        warm = keep.tile([P, 1], F32, name="warm")
        nc.scalar.activation(warm[:], half_col[:], ACT.Ln)
        xs = keep.tile([P, T], U8, name="xs", tag="xs", align_bytes=64)
        nc.vector.memset(xs[:].bitcast(I32), 0)
        l_two = load_list("l_two", two)
        l_offs = load_list("l_offs", offs)
        for q in range(4):
            nc.sync.dma_start(xs[32 * q : 32 * q + 4, :].bitcast(I32), x_scales[0, 4 * q : 4 * q + 4, :].bitcast(I32))
        gi_rows = load_gain("gi_rows", gi)
        xw = keep.tile([P, T], I32, name="xw")
        nc.sync.dma_start(xw[:], x_words[0].rearrange("p n t -> p (n t)").bitcast(I32))
        l3 = load_list("l3", n3)
        wb_parts = ((0, P), (P, HALF), (HALF, W))
        wb_raw = [load_weight_part("wb_raw%d" % c0, wb, c0, c1, "wb_raw%d" % c0) for c0, c1 in wb_parts]
        gt_rows = load_gain("gt_rows", gt)
        l2 = load_list("l2", n2)
        l1 = load_list("l1", n1)
        l5 = load_list("l5", n5)
        l6 = load_list("l6", n6)
        l4 = load_list("l4", n4)
        ident = keep.tile([P, P], F32, name="ident")
        make_identity(nc, ident[:])

        def pick_scales(name, lst):
            picked = keep.tile([P, W], U8, name=name + "_sp", tag=name + "_sp", align_bytes=64)
            nc.vector.tensor_copy(picked[:], xs[:].indirect(lst[:]))
            dealt = keep.tile([P, W], U8, name=name + "_s", align_bytes=64)
            nc.vector.tensor_copy(
                dealt[:].bitcast(I32).rearrange("p (t b e) -> p t b e", t=PACK, e=RUN // 4),
                picked[:].bitcast(I32).rearrange("p (b t e) -> p t b e", t=PACK, e=RUN // 4),
            )
            return dealt

        def pick_words(name, lst, tag):
            dealt = keep.tile([P, W], U32, name=name + "_w", tag=tag, align_bytes=64)
            nc.vector.tensor_copy(
                dealt[:].rearrange("p (t b c) -> p b t c", t=PACK, c=RUN), xw[:].bitcast(U32).indirect(lst[:])
            )
            return dealt

        def interleave(copy, grouped, planes):
            copy(grouped.rearrange("p (c i) j -> p c j i", i=PACK), planes.rearrange("p j (c i) -> p c j i", i=PACK))

        def cast_weight(name, raw):
            grouped = keep.tile([P, W, PACK], BF16, name=name + "_bf", tag="xb_w", align_bytes=64)
            for h in range(2):
                interleave(nc.scalar.copy, grouped[:, h * HALF : (h + 1) * HALF, :], raw[h][:])
            return grouped

        def quantize(name, grouped, width):
            codes = keep.tile([P, width], U32, name=name + "_q", align_bytes=64)
            scales = keep.tile([P, width], U8, name=name + "_qs", align_bytes=64)
            nc.vector.quantize_mx(out=codes[:].bitcast(FP8X4), scales=scales[:], in_=grouped[:].rearrange("p c j -> p (c j)"))
            return codes, scales

        def multiply(dst, lhs, lhs_s, rhs, rhs_s):
            nc.tensor.matmul_mx(
                out=dst, lhsT=lhs.bitcast(FP8X4), lhsT_scale=lhs_s, rhs=rhs.bitcast(FP8X4), rhs_scale=rhs_s,
                start=True, stop=True,
            )

        def product(tag, lhs, lhs_s, rhs, rhs_s):
            bank = psum.tile([P, W], F32, name=tag, tag=tag)
            multiply(bank[:], lhs, lhs_s, rhs, rhs_s)
            return bank

        xb_s = pick_scales("xb", l_two)
        xa_s = pick_scales("xa", l_offs)
        wa_raw = [load_weight_part("wa_raw%d" % h, wa, h * HALF, (h + 1) * HALF, ("xb_sp", "xs")[h]) for h in range(2)]
        xb_w = pick_words("xb", l_two, "xb_w")
        halves = [slice(h * HALF, (h + 1) * HALF) for h in range(2)]
        wb_q = keep.tile([P, W], U32, name="wb_q", align_bytes=64)
        wb_s = keep.tile([P, W], U8, name="wb_qs", align_bytes=64)

        def turn_gain(name, rows, tag):
            turned = psum.tile([P, P], F32, name=name, tag=tag)
            nc.tensor.transpose(turned[:], rows[:], ident[:])
            return turned[:, 0:PACK]

        gi_col = turn_gain("gi_col", gi_rows, "a0")
        gi_abs = keep.tile([P, PACK], F32, name="gi_abs")
        nc.scalar.activation(gi_abs[:], gi_col, ACT.Abs)
        gi_half = keep.tile([P, PACK], F32, name="gi_half")
        nc.scalar.activation(gi_half[:], gi_col, ACT.Abs, scale=0.5)
        gi_sign = keep.tile([P, PACK], F32, name="gi_sign")
        nc.scalar.activation(gi_sign[:], gi_col, ACT.Sign)
        gi_unit = keep.tile([P, PACK], F32, name="gi_unit")
        nc.scalar.activation(gi_unit[:], gi_sign[:], ACT.Sign, bias=half_col[:])

        cols = [slice(t * P, (t + 1) * P) for t in range(PACK)]
        b_bank = [psum.tile([P, W], F32, name="b%d" % t, tag="b%d" % t) for t in range(PACK)]

        a_abs = [keep.tile([P, 2 * W], F32, name="a_abs%d" % t) for t in range(PACK)]
        a_num = [keep.tile([P, 2 * W], F32, name="a_num%d" % t) for t in range(PACK)]
        ds = [keep.tile([P, 2 * W], F32, name="ds%d" % t) for t in range(2)]

        def send(t, c0, c1, tag):
            rl = keep.tile([P, c1 - c0], F32, name="rl%d_%d" % (t, c0), tag=tag, align_bytes=64)
            nc.scalar.activation(rl[:], b_bank[t][:, c0:c1], ACT.Relu, scale=gi_abs[:, t : t + 1])
            nc.vector.tensor_copy(ds[t][:].indirect(l3[:, c0 // 16 : c1 // 16]), rl[:])

        for raw, (c0, c1) in zip(wb_raw, wb_parts):
            wb_bf = keep.tile([P, c1 - c0, PACK], BF16, name="wb_bf%d" % c0, tag="wb_bf%d" % c0, align_bytes=64)
            interleave(nc.scalar.copy, wb_bf[:], raw[:])
            nc.vector.quantize_mx(
                out=wb_q[:, c0:c1].bitcast(FP8X4), scales=wb_s[:, c0:c1], in_=wb_bf[:].rearrange("p c j -> p (c j)")
            )
            multiply(b_bank[0][:, c0:c1], xb_w[:, cols[0]], xb_s[:, cols[0]], wb_q[:, c0:c1], wb_s[:, c0:c1])
            send(0, c0, c1, "rl0_%d" % c0)
        xa_w = pick_words("xa", l_offs, "wb_bf0")
        for t in range(1, PACK):
            multiply(b_bank[t][:], xb_w[:, cols[t]], xb_s[:, cols[t]], wb_q[:], wb_s[:])
        send(1, 0, HALF, "rl1")
        wa_bf = cast_weight("wa", wa_raw)
        wa_q, wa_s = quantize("wa", wa_bf, W)
        send(1, HALF, W, "xs")
        gt_col = turn_gain("gt_col", gt_rows, "a1")
        gt_signed = keep.tile([P, PACK], F32, name="gt_signed")
        for t in range(PACK):
            nc.scalar.activation(gt_signed[:, t : t + 1], gt_col[:, t : t + 1], ACT.Copy, scale=gi_unit[:, t : t + 1])
        a_bank = [product("a%d" % t, xa_w[:, cols[t]], xa_s[:, cols[t]], wa_q[:], wa_s[:]) for t in range(PACK)]
        den = keep.tile([P, PACK, W], F32, name="den")
        for t in range(PACK):
            nc.scalar.activation(a_abs[t][:, 0:W], a_bank[t][:], ACT.Abs)
            own = keep.tile([P, W], F32, name="own%d" % t, tag="own%d" % t, align_bytes=64)
            nc.scalar.activation(own[:], a_bank[t][:], ACT.Abs)
            nc.vector.tensor_tensor(den[:, t, :], a_abs[t][:].indirect(l2[:]), own[:], ALU.add)
        ds.extend([a_abs[3], keep.tile([P, 2 * W], F32, name="ds3", tag="own3", align_bytes=64)])
        send(2, 0, W, "xb_sp")
        send(3, 0, W, "xb_w")
        for t in range(PACK):
            nc.scalar.activation(a_num[t][:, 0:W], a_bank[t][:], ACT.Copy, scale=gt_signed[:, t : t + 1])
        log_den = keep.tile([P, PACK, W], F32, name="log_den", tag="log_den", align_bytes=64)
        nc.scalar.activation(log_den[:], den[:], ACT.Ln, bias=half_col[:])
        z2_bf = keep.tile([P, PACK, W], BF16, name="z2_bf", tag="xb_sp", align_bytes=64)

        def finish_z2(t):
            nc.vector.scalar_tensor_tensor(
                z2_bf[:, t, :], b_bank[t][:], gi_half[:, t : t + 1], ds[t][:, 0:W], ALU.mult, ALU.subtract
            )

        rec = keep.tile([P, PACK, W], F32, name="rec")
        nc.scalar.activation(rec[:], log_den[:], ACT.Exp, scale=-1.0)
        for t in range(PACK):
            finish_z2(t)
        z2_grouped = keep.tile([P, W, PACK], BF16, name="z2_grouped", tag="log_den", align_bytes=64)
        z2_q = keep.tile([P, W], U32, name="z2_q", align_bytes=64)
        z2_s = keep.tile([P, W], U8, name="z2_s", align_bytes=64)
        for h in range(2):
            interleave(nc.scalar.copy, z2_grouped[:, halves[h], :], z2_bf[:, :, halves[h]])
            nc.vector.quantize_mx(
                out=z2_q[:, halves[h]].bitcast(FP8X4),
                scales=z2_s[:, halves[h]],
                in_=z2_grouped[:, halves[h], :].rearrange("p c j -> p (c j)"),
            )
        z_grouped = keep.tile([P, PACK, P, PACK], BF16, name="z_grouped", align_bytes=64)
        early = 3 * W // 4
        parts = []
        for c0, c1 in ((0, early), (early, W)):
            z = keep.tile([P, PACK, c1 - c0], F32, name="z%d" % c0)
            for t in range(PACK):
                nc.vector.tensor_tensor(
                    z[:, t, :], a_num[t][:].indirect(l1[:, c0 // 16 : c1 // 16]), rec[:, t, c0:c1], ALU.mult
                )
            parts.append(
                (
                    z_grouped[:, :, c0 // PACK : c1 // PACK, :].rearrange("p u m t -> p m t u"),
                    z[:].rearrange("p t (m u) -> p m t u", u=PACK),
                )
            )
        nc.scalar.copy(*parts[0])
        nc.vector.tensor_copy(*parts[1])

        out_rows = out.rearrange("(p u) c -> p u c", u=PACK)
        win, banks = a_num, []
        turned_tiles = 2
        z_q = keep.tile([P, W], U32, name="z_q", align_bytes=64)
        z_s = keep.tile([P, W], U8, name="z_s", align_bytes=64)
        for u0, u1 in ((0, 1), (1, 2), (2, 4)):
            nc.vector.quantize_mx(
                out=z_q[:, u0 * P : u1 * P].bitcast(FP8X4),
                scales=z_s[:, u0 * P : u1 * P],
                in_=z_grouped[:, u0:u1].rearrange("p u m t -> p (u m t)"),
            )
        for u in range(PACK):
            bank = product("a%d" % u, z_q[:, cols[u]], z_s[:, cols[u]], z2_q[:], z2_s[:])
            nc.scalar.activation(win[u][:, 0:W], bank[:], ACT.Copy, scale=-0.0625)
            banks.append(bank)

        direct = range(turned_tiles, PACK)
        cv = keep.tile([P, len(direct), W], F32, name="cv")
        for i, u in enumerate(direct):
            nc.scalar.activation(cv[:, i, :], banks[u][:], ACT.Copy, scale=-0.0625)
        g5 = [keep.tile([P, W], F32, name="g5_%d" % u) for u in range(turned_tiles)]
        rest = keep.tile([P, PACK, W], F32, name="rest")

        def fetch5(u):
            nc.vector.tensor_copy(g5[u][:], win[u][:].indirect(l5[:]))

        def rest_on_tensor(u):
            d65 = keep.tile([P, W], F32, name="d65_%d" % u)
            nc.vector.tensor_tensor(d65[:], win[u][:].indirect(l6[:]), g5[u][:], ALU.subtract)
            minus_cv = keep.tile([P, W], F32, name="minus_cv%d" % u)
            nc.scalar.activation(minus_cv[:], banks[u][:], ACT.Copy, scale=0.0625)
            excess = keep.tile([P, W], F32, name="excess%d" % u)
            nc.scalar.activation(excess[:], d65[:], ACT.Relu)
            turned = psum.tile([P, W], F32, name="turned%d" % u, tag="b%d" % (u % 2))
            terms = (minus_cv, g5[u], excess)
            for k in range(PACK):
                for i, term in enumerate(terms):
                    nc.tensor.matmul(
                        turned[:, cols[k]], term[:, cols[k]], ident[:], start=i == 0, stop=i == len(terms) - 1,
                        is_transpose=True,
                    )
            turned_sb = keep.tile([P, W], F32, name="turned_sb%d" % u)
            nc.scalar.copy(turned_sb[:], turned[:])
            back = psum.tile([P, W], F32, name="back%d" % u, tag="b%d" % (2 + u % 2))
            for k in range(PACK):
                nc.tensor.transpose(back[:, cols[k]], turned_sb[:, cols[k]], ident[:])
            nc.scalar.copy(rest[:, u, :], back[:])

        for u in range(turned_tiles):
            fetch5(u)
        for u in range(turned_tiles):
            rest_on_tensor(u)

        d5 = keep.tile([P, len(direct), W], F32, name="d5")
        d6 = keep.tile([P, len(direct), W], F32, name="d6")
        for i, u in enumerate(direct):
            nc.vector.tensor_tensor(d5[:, i, :], win[u][:].indirect(l5[:]), cv[:, i, :], ALU.subtract)
            nc.vector.tensor_tensor(d6[:, i, :], win[u][:].indirect(l6[:]), cv[:, i, :], ALU.subtract)
        nc.vector.tensor_tensor(rest[:, turned_tiles:PACK, :], d5[:], d6[:], ALU.max)
        for u in (2, 3, 0, 1):
            pieces = 2 if u == 1 else 1
            width = W // pieces
            for h in range(pieces):
                span = slice(h * width, (h + 1) * width)
                res = keep.tile([P, width], F32, name="res%d_%d" % (u, h))
                nc.vector.tensor_tensor(
                    res[:], win[u][:].indirect(l4[:, h * width // 16 : (h + 1) * width // 16]), rest[:, u, span],
                    ALU.subtract,
                )
                nc.sync.dma_start(out_rows[:, u, span], res[:])
